import numpy as np
import ml_dtypes


def mxq(x, axis, fmt="e4m3"):
    dtype, down = {"e4m3": (ml_dtypes.float8_e4m3fn, 7), "e5m2": (ml_dtypes.float8_e5m2, 14)}[fmt]
    v = np.moveaxis(np.asarray(x, np.float32).astype(ml_dtypes.bfloat16).astype(np.float64), axis, -1)
    blocks = v.reshape(v.shape[:-1] + (-1, 32))
    amax = np.abs(blocks).max(-1, keepdims=True)
    byte = np.maximum(np.where(amax > 0, np.frexp(amax)[1] - 1 + 127, 0) - down, 1)
    scale = np.exp2(byte - 127.0)
    codes = (blocks / scale).astype(np.float32).astype(dtype).astype(np.float64)
    return np.moveaxis((codes * scale).reshape(v.shape), -1, axis)


WIDE = False


def mx_kscale(k):
    if not WIDE:
        return np.ones(k)
    levels = np.array([10, -10, 5, -5, 0])
    if k % 512:
        return np.exp2(np.random.permutation(np.resize(levels, k // 32))).repeat(32)
    a = np.empty((k // 512, 16))
    for p in range(k // 512):
        a[p, :8] = np.random.permutation(np.resize(levels, 8))
        for g in range(8):
            far = levels[np.abs(levels - a[p, g]) >= 10]
            a[p, g + 8] = far[np.random.randint(len(far))]
    return np.exp2(a.ravel()).repeat(32)


def f64(x):
    return np.asarray(x).astype(np.float64)


def striped(idx):
    return np.tile(idx.reshape(-1, 16).T, (8, 1)).astype(np.uint16)


def unstriped(offs):
    return offs[:16].T.reshape(-1).astype(np.int64)


def pack_weight(w):
    k, n = w.shape
    w = f64(np.asarray(w, np.float32).astype(ml_dtypes.bfloat16)).reshape(k // 32, 32, n)
    amax = np.abs(w).max(1)
    byte = np.clip(np.where(amax > 0, np.frexp(amax)[1] - 1 + 127 - 7, 1), 1, 254)
    scaled = (w * np.exp2(127.0 - byte)[:, None, :]).reshape(k, n).astype(np.float32)
    words = np.ascontiguousarray(scaled.reshape(k // 512, 128, 4, n).transpose(0, 1, 3, 2)).astype(ml_dtypes.float8_e4m3fn).view(np.uint8)
    return words, np.ascontiguousarray(byte.astype(np.uint8).reshape(k // 512, 16, n))


def unpack_weight(words, scales):
    g, p, n, _ = words.shape
    vals = np.ascontiguousarray(words).view(ml_dtypes.float8_e4m3fn).astype(np.float64) * np.repeat(np.exp2(scales.astype(np.float64) - 127.0), 8, axis=1)[..., None]
    return vals.transpose(0, 1, 3, 2).reshape(g * 512, n)


def relu(v):
    return np.maximum(v, 0.0)

def planes(y):
    n, m = y.shape
    v = y.astype(np.float32).astype(ml_dtypes.bfloat16).astype(np.float64).reshape(n // 32, 32, m)
    top = np.abs(v).max(1)
    byte = np.clip(np.where(top > 0, np.frexp(top)[1] - 1 + 127 - 7, 1), 1, 254)
    codes = (v * np.exp2(127.0 - byte)[:, None, :]).reshape(n, m).astype(np.float32).astype(ml_dtypes.float8_e4m3fn).view(np.uint8)
    words = codes.reshape(n // 512, 128, 4, m).transpose(0, 1, 3, 2)
    return np.ascontiguousarray(words), np.ascontiguousarray(byte.astype(np.uint8).reshape(n // 512, 16, m))


K, T, D, N = 512, 512, 3, 512
P = 2 ** 7


def setup_inputs():
    n = np.random.standard_normal
    s = mx_kscale(K)[:, None]
    packed_xT = pack_weight(n((K, T)) * s)
    return {
        "x_words": packed_xT[0],
        "x_scales": packed_xT[1],
        "w1": (n((K, N)) / np.sqrt(K) / s).astype(np.float32),
        "score": np.tile(np.random.standard_normal((D, 1, T)), (1, P, 1)).astype(np.float32),
        "pos1": striped(np.random.permutation(T)),
        "pos2": striped(np.random.permutation(T)),
        "pos3": striped(np.random.permutation(T)),
    }


def reference(x_words, x_scales, w1, score, pos1, pos2, pos3):
    xq = unpack_weight(x_words, x_scales)
    y = mxq(f64(w1), 0, "e4m3").T @ xq
    e0 = np.exp(f64(score)[0, :1])
    e1 = np.exp(f64(score)[1, :1])
    e2 = np.exp(f64(score)[2, :1])
    num = y[:, unstriped(pos1)] * e0 + y[:, unstriped(pos2)] * e1 + y[:, unstriped(pos3)] * e2
    den = e0 + e1 + e2
    out_0 = relu(num / den)
    return (out_0,) + planes(out_0)

@@ -1,0 +1,220 @@
+from contextlib import ExitStack
+
+import concourse.mybir as mybir
+from concourse.masks import make_identity
+
+K, T, D, N = 512, 512, 3, 512
+P = 128
+PACK = 4
+BLOCKS = N // P
+FLOPS = 2 * K * T * N
+BYTES = K * T + K * T // 32 + 4 * K * N + 4 * D * T + D * P * (T // 16) * 2 + 4 * N * T + N * T + N * T // 32
+
+F32 = mybir.dt.float32
+BF16 = mybir.dt.bfloat16
+I32 = mybir.dt.int32
+U32 = mybir.dt.uint32
+U16 = mybir.dt.uint16
+U8 = mybir.dt.uint8
+FP8X4 = mybir.dt.float8_e4m3fn_x4
+ALU = mybir.AluOpType
+ACT = mybir.ActivationFunctionType
+AXIS = mybir.AxisListType
+
+
+def tile_picked_wgatv_relu_lo_kernel(
+    tc, x_words, x_scales, w1, score, pos1, pos2, pos3, out_0, out_1, out_2
+):
+    nc = tc.nc
+    with ExitStack() as ctx:
+        sb = ctx.enter_context(tc.tile_pool(name="sb", bufs=1))
+        ps = ctx.enter_context(tc.psum_pool(name="ps", bufs=1))
+
+        def bank(i, name):
+            return ps.tile([P, T], F32, name=name, tag="bank%d" % i)
+
+        s_small = sb.tile([P, D, 8], F32, name="s_small")
+        nc.sync.dma_start(out=s_small[:, :, 0:PACK], in_=score[:, 0, :].rearrange("d (n c) -> n d c", c=PACK))
+        w_raw = [sb.tile([P, PACK, P], F32, name="w_raw%d" % b) for b in range(BLOCKS)]
+
+        def load_w(b):
+            nc.sync.dma_start(out=w_raw[b][:], in_=w1[:, b * P:(b + 1) * P].rearrange("(p j) m -> p j m", j=PACK))
+
+        load_w(0)
+        xw = sb.tile([P, T], U32, name="xw", tag="late", align_bytes=64)
+        nc.sync.dma_start(out=xw[:].bitcast(I32), in_=x_words[0].rearrange("p c r -> p (c r)").bitcast(I32))
+        xs = sb.tile([P, T], U8, name="xs", tag="late2", align_bytes=64)
+        for q in range(4):
+            nc.scalar.dma_start(
+                out=xs[32 * q:32 * (q + 1), :].bitcast(I32),
+                in_=x_scales[0, 4 * q:4 * (q + 1), :].bitcast(I32).partition_broadcast(8),
+            )
+        pos = [sb.tile([P, T // 16], U16, name="pos%d" % d) for d in range(D)]
+        nc.sync.dma_start(pos[0][:], pos1)
+        load_w(1)
+        nc.sync.dma_start(pos[1][:], pos2)
+        nc.sync.dma_start(pos[2][:], pos3)
+        load_w(2)
+        load_w(3)
+
+        ident = sb.tile([P, P], F32, name="ident")
+        make_identity(nc, ident[:])
+
+        warm_in = sb.tile([P, 1], F32, name="warm_in")
+        warm_out = sb.tile([P, 1], F32, name="warm_out")
+        nc.vector.memset(warm_in[:], 0.0)
+        nc.scalar.activation(warm_out[:], warm_in[:], ACT.Exp)
+
+        s_dc = s_small[:, :, 0:PACK]
+        top = sb.tile([P, PACK], F32, name="top")
+        nc.vector.tensor_reduce(top[:], s_dc.rearrange("p d c -> p c d"), AXIS.X, ALU.max)
+        z = sb.tile([P, D, PACK], F32, name="z")
+        nc.vector.tensor_tensor(z[:], s_dc, top[:].unsqueeze(1).to_broadcast([P, D, PACK]), ALU.subtract)
+        e = sb.tile([P, D, PACK], F32, name="e")
+        nc.scalar.activation(e[:], z[:], ACT.Exp)
+        den = sb.tile([P, PACK], F32, name="den")
+        nc.vector.tensor_reduce(den[:], e[:].rearrange("p d c -> p c d"), AXIS.X, ALU.add)
+        rden = sb.tile([P, PACK], F32, name="rden")
+        nc.vector.reciprocal(rden[:], den[:])
+        a_small = sb.tile([P, D, PACK], F32, name="a_small")
+        nc.vector.tensor_tensor(a_small[:], e[:], rden[:].unsqueeze(1).to_broadcast([P, D, PACK]), ALU.mult)
+
+        w_bf = [sb.tile([P, P * PACK], BF16, name="w_bf%d" % b, align_bytes=64) for b in range(BLOCKS)]
+        w_q = [sb.tile([P, P], U32, name="w_q%d" % b, align_bytes=64) for b in range(BLOCKS)]
+        w_s = [sb.tile([P, P], U8, name="w_s%d" % b, align_bytes=64) for b in range(BLOCKS)]
+        y = [sb.tile([P, T], F32, name="y%d" % b) for b in range(BLOCKS)]
+
+        def cast_w(b):
+            dst = w_bf[b][:].rearrange("p (g i j) -> p g j i", i=4, j=PACK)
+            src = w_raw[b][:].rearrange("p j (g i) -> p g j i", i=4)
+            if b == 0:
+                nc.vector.tensor_copy(dst, src)
+            else:
+                nc.scalar.copy(dst, src)
+
+        def project(b):
+            nc.vector.quantize_mx(out=w_q[b][:].bitcast(FP8X4), scales=w_s[b][:], in_=w_bf[b][:])
+            acc = bank(3 + b, "acc%d" % b)
+            nc.tensor.matmul_mx(
+                out=acc[:], lhsT=w_q[b][:].bitcast(FP8X4), lhsT_scale=w_s[b][:],
+                rhs=xw[:].bitcast(FP8X4), rhs_scale=xs[:], start=True, stop=True,
+            )
+            nc.scalar.copy(y[b][:], acc[:])
+
+        cast_w(0)
+        cast_w(1)
+        project(0)
+
+        a_bank = [bank(d, "a_bank%d" % d) for d in range(D)]
+        HALF = T // 2
+        a_first = [sb.tile([P, HALF], F32, name="a_first%d" % d) for d in range(D)]
+
+        def a_half(d, h):
+            return a_bank[d][:].rearrange("p (c n) -> p n c", c=PACK)[:, h * 64:(h + 1) * 64, :]
+
+        for d in range(D):
+            for c in range(PACK):
+                nc.tensor.transpose(
+                    a_bank[d][:, c * P:(c + 1) * P], a_small[:, d, c:c + 1].to_broadcast([P, P]), ident[:]
+                )
+            dst = a_first[d][:].rearrange("p (n c) -> p n c", c=PACK)
+            if d == 0:
+                nc.vector.tensor_copy(dst, a_half(d, 0))
+            else:
+                nc.scalar.copy(dst, a_half(d, 0))
+
+        def gather(b, d, v0, width, weights):
+            h = sb.tile([P, width], F32, name="h_%d_%d_%d" % (v0, b, d))
+            nc.vector.tensor_tensor(
+                h[:], y[b][:].indirect(pos[d][:, v0 // 16:(v0 + width) // 16]), weights, ALU.mult
+            )
+            return h
+
+        def turn_add(dst, src, d):
+            nc.tensor.matmul(dst, src, ident[:], start=(d == 0), stop=(d == D - 1), is_transpose=True)
+
+        planes_s = sb.tile([P, T], U8, name="planes_s", align_bytes=64)
+        out_rows = out_0.rearrange("(p t) v -> p t v", t=PACK)
+        out_words = out_1[0].rearrange("p c r -> p (c r)").bitcast(I32)
+        sums = {c: sb.tile([P, PACK, P], F32, name="sums%d" % c)[:] for c in (2, 3)}
+
+        def relu_out(c, src, b0, b1):
+            nc.scalar.activation(
+                sums[c][:, :, 32 * b0:32 * b1],
+                src[:, P * b0:P * b1].rearrange("p (q t) -> p t q", t=PACK),
+                ACT.Relu,
+            )
+
+        def finish(c, bank_no, last):
+            back = bank(bank_no, "back%d" % c)
+            for t in range(PACK):
+                nc.tensor.transpose(back[:, t * P:(t + 1) * P], sums[c][:, t, :], ident[:])
+            res = sb.tile([P, PACK, P], F32, name="res%d" % c)
+            res_bf = sb.tile([P, P * PACK], BF16, name="res_bf%d" % c, align_bytes=64)
+            words = sb.tile([P, P], U32, name="words%d" % c, align_bytes=64)
+            dst = res_bf[:].rearrange("p (v t) -> p v t", t=PACK)
+            src = back[:].rearrange("p (t v) -> p v t", t=PACK)
+            if last:
+                nc.vector.tensor_copy(dst, src)
+            nc.scalar.copy(res[:].rearrange("p t v -> p (t v)"), back[:])
+            nc.sync.dma_start(out=out_rows[:, :, c * P:(c + 1) * P], in_=res[:])
+            if not last:
+                nc.scalar.copy(dst, src)
+            nc.vector.quantize_mx(
+                out=words[:].bitcast(FP8X4), scales=planes_s[:, c * P:(c + 1) * P], in_=res_bf[:]
+            )
+            nc.sync.dma_start(out=out_words[:, c * P:(c + 1) * P], in_=words[:].bitcast(I32))
+
+        sum_first = []
+        for b in range(BLOCKS):
+            if b + 2 < BLOCKS:
+                cast_w(b + 2)
+            if b + 1 < BLOCKS:
+                project(b + 1)
+            sum_first.append(bank(3 + (b + 1) % BLOCKS, "sum_first%d" % b))
+            hs = [gather(b, d, 0, HALF, a_first[d][:]) for d in range(D)]
+            for c in range(2):
+                for d in range(D):
+                    turn_add(sum_first[b][:, c * P:(c + 1) * P], hs[d][:, c * P:(c + 1) * P], d)
+            if b + 2 == BLOCKS:
+                a_second = sb.tile([P, D, HALF], F32, name="a_second", tag="late", align_bytes=64)
+                for d in range(D):
+                    nc.scalar.copy(a_second[:, d, :].rearrange("p (n c) -> p n c", c=PACK), a_half(d, 1))
+                sums_first = sb.tile([P, 2, PACK, P], F32, name="sums_first", tag="late2", align_bytes=64)
+                sums[0] = sums_first[:, 0]
+                sums[1] = sums_first[:, 1]
+            for done in ([0, 1, 2] if b + 2 == BLOCKS else [3] if b + 1 == BLOCKS else []):
+                nc.scalar.activation(
+                    sums_first[:, :, :, 32 * done:32 * (done + 1)],
+                    sum_first[done][:, 0:HALF].rearrange("p (c q t) -> p c t q", c=2, t=PACK),
+                    ACT.Relu,
+                )
+        finish(0, 7, False)
+        finish(1, 0, False)
+
+        sum2 = bank(3, "sum2")
+        for b in range(BLOCKS):
+            for d in range(D):
+                h = gather(b, d, 2 * P, P, a_second[:, d, 0:P])
+                turn_add(sum2[:, b * P:(b + 1) * P], h[:], d)
+        relu_out(2, sum2, 0, BLOCKS)
+        finish(2, 1, False)
+
+        sum3 = bank(3, "sum3")
+        sum3_last = bank(4, "sum3_last")
+        for b in range(BLOCKS):
+            for d in range(D):
+                h = gather(b, d, 3 * P, P, a_second[:, d, P:2 * P])
+                dst = sum3_last if b == BLOCKS - 1 else sum3
+                turn_add(dst[:, b * P:(b + 1) * P], h[:], d)
+            if b == BLOCKS - 2:
+                relu_out(3, sum3, 0, BLOCKS - 1)
+        relu_out(3, sum3_last, BLOCKS - 1, BLOCKS)
+        finish(3, 2, True)
+
+        for q in range(4):
+            eng = nc.scalar if q % 2 else nc.sync
+            eng.dma_start(
+                out=out_2[0, 4 * q:4 * (q + 1), :].bitcast(I32),
+                in_=planes_s[32 * q:32 * q + 4, :].bitcast(I32),
+            )

@@ -10,6 +10,10 @@ BLOCKS = N // P
 FLOPS = 2 * K * T * N
 BYTES = K * T + K * T // 32 + 4 * K * N + 4 * D * T + D * P * (T // 16) * 2 + 4 * N * T + N * T + N * T // 32
 
+ROW_STEP = 9
+D_STEP = 60
+RING = 4
+
 F32 = mybir.dt.float32
 BF16 = mybir.dt.bfloat16
 I32 = mybir.dt.int32
@@ -33,17 +37,19 @@ def tile_picked_wgatv_relu_lo_kernel(
         def bank(i, name):
             return ps.tile([P, T], F32, name=name, tag="bank%d" % i)
 
-        s_small = sb.tile([P, D, 8], F32, name="s_small")
-        nc.sync.dma_start(out=s_small[:, :, 0:PACK], in_=score[:, 0, :].rearrange("d (n c) -> n d c", c=PACK))
+        s_rows = sb.tile([P, P], F32, name="s_rows")
+        nc.gpsimd.dma_start(
+            out=s_rows[:], in_=score.rearrange("d p (c n) -> (d p c) n", n=P)[0:ROW_STEP * P:ROW_STEP, :]
+        )
         w_raw = [sb.tile([P, PACK, P], F32, name="w_raw%d" % b) for b in range(BLOCKS)]
 
         def load_w(b):
             nc.sync.dma_start(out=w_raw[b][:], in_=w1[:, b * P:(b + 1) * P].rearrange("(p j) m -> p j m", j=PACK))
 
         load_w(0)
-        xw = sb.tile([P, T], U32, name="xw", tag="late", align_bytes=64)
+        xw = sb.tile([P, T], U32, name="xw", align_bytes=64)
         nc.sync.dma_start(out=xw[:].bitcast(I32), in_=x_words[0].rearrange("p c r -> p (c r)").bitcast(I32))
-        xs = sb.tile([P, T], U8, name="xs", tag="late2", align_bytes=64)
+        xs = sb.tile([P, T], U8, name="xs", align_bytes=64)
         for q in range(4):
             nc.scalar.dma_start(
                 out=xs[32 * q:32 * (q + 1), :].bitcast(I32),
@@ -52,10 +58,10 @@ def tile_picked_wgatv_relu_lo_kernel(
         pos = [sb.tile([P, T // 16], U16, name="pos%d" % d) for d in range(D)]
         nc.sync.dma_start(pos[0][:], pos1)
         load_w(1)
-        nc.sync.dma_start(pos[1][:], pos2)
-        nc.sync.dma_start(pos[2][:], pos3)
         load_w(2)
         load_w(3)
+        nc.sync.dma_start(pos[1][:], pos2)
+        nc.sync.dma_start(pos[2][:], pos3)
 
         ident = sb.tile([P, P], F32, name="ident")
         make_identity(nc, ident[:])
@@ -65,7 +71,44 @@ def tile_picked_wgatv_relu_lo_kernel(
         nc.vector.memset(warm_in[:], 0.0)
         nc.scalar.activation(warm_out[:], warm_in[:], ACT.Exp)
 
-        s_dc = s_small[:, :, 0:PACK]
+        w_bf = [sb.tile([P, P * PACK], BF16, name="w_bf%d" % b, align_bytes=64) for b in range(BLOCKS)]
+        w_q = [sb.tile([P, P], U32, name="w_q%d" % b, align_bytes=64) for b in range(BLOCKS)]
+        w_s = [sb.tile([P, P], U8, name="w_s%d" % b, align_bytes=64) for b in range(BLOCKS)]
+        y = [sb.tile([P, T], F32, name="y%d" % b) for b in range(BLOCKS)]
+
+        def cast_w(b):
+            dst = w_bf[b][:].rearrange("p (g i j) -> p g j i", i=4, j=PACK)
+            src = w_raw[b][:].rearrange("p j (g i) -> p g j i", i=4)
+            if b < 2:
+                nc.vector.tensor_copy(dst, src)
+            else:
+                nc.scalar.copy(dst, src)
+
+        def product(acc, b, cols):
+            nc.tensor.matmul_mx(
+                out=acc, lhsT=w_q[b][:].bitcast(FP8X4), lhsT_scale=w_s[b][:],
+                rhs=xw[:, cols].bitcast(FP8X4), rhs_scale=xs[:, cols], start=True, stop=True,
+            )
+
+        def project(b):
+            nc.vector.quantize_mx(out=w_q[b][:].bitcast(FP8X4), scales=w_s[b][:], in_=w_bf[b][:])
+            if b == 0:
+                for h, copy in enumerate((nc.scalar.copy, nc.vector.tensor_copy)):
+                    cols = slice(h * T // 2, (h + 1) * T // 2)
+                    acc = bank(5 + h, "acc0_%d" % h)
+                    product(acc[:, 0:T // 2], b, cols)
+                    copy(y[b][:, cols], acc[:, 0:T // 2])
+            else:
+                acc = bank(5 + (b + 1) % 2, "acc%d" % b)
+                product(acc[:], b, slice(0, T))
+                nc.scalar.copy(y[b][:], acc[:])
+
+        cast_w(0)
+        project(0)
+
+        s_bank = bank(7, "s_bank")
+        nc.tensor.transpose(s_bank[:, 0:P], s_rows[:], ident[:])
+        s_dc = s_bank[:, 0:D * D_STEP].rearrange("p (d r) -> p d r", r=D_STEP)[:, :, 0:PACK]
         top = sb.tile([P, PACK], F32, name="top")
         nc.vector.tensor_reduce(top[:], s_dc.rearrange("p d c -> p c d"), AXIS.X, ALU.max)
         z = sb.tile([P, D, PACK], F32, name="z")
@@ -76,141 +119,123 @@ def tile_picked_wgatv_relu_lo_kernel(
         nc.vector.tensor_reduce(den[:], e[:].rearrange("p d c -> p c d"), AXIS.X, ALU.add)
         rden = sb.tile([P, PACK], F32, name="rden")
         nc.vector.reciprocal(rden[:], den[:])
-        a_small = sb.tile([P, D, PACK], F32, name="a_small")
-        nc.vector.tensor_tensor(a_small[:], e[:], rden[:].unsqueeze(1).to_broadcast([P, D, PACK]), ALU.mult)
+        a = sb.tile([P, D, PACK], F32, name="a")
+        nc.vector.tensor_tensor(a[:], e[:], rden[:].unsqueeze(1).to_broadcast([P, D, PACK]), ALU.mult)
 
-        w_bf = [sb.tile([P, P * PACK], BF16, name="w_bf%d" % b, align_bytes=64) for b in range(BLOCKS)]
-        w_q = [sb.tile([P, P], U32, name="w_q%d" % b, align_bytes=64) for b in range(BLOCKS)]
-        w_s = [sb.tile([P, P], U8, name="w_s%d" % b, align_bytes=64) for b in range(BLOCKS)]
-        y = [sb.tile([P, T], F32, name="y%d" % b) for b in range(BLOCKS)]
-
-        def cast_w(b):
-            dst = w_bf[b][:].rearrange("p (g i j) -> p g j i", i=4, j=PACK)
-            src = w_raw[b][:].rearrange("p j (g i) -> p g j i", i=4)
-            if b == 0:
-                nc.vector.tensor_copy(dst, src)
-            else:
-                nc.scalar.copy(dst, src)
-
-        def project(b):
-            nc.vector.quantize_mx(out=w_q[b][:].bitcast(FP8X4), scales=w_s[b][:], in_=w_bf[b][:])
-            acc = bank(3 + b, "acc%d" % b)
-            nc.tensor.matmul_mx(
-                out=acc[:], lhsT=w_q[b][:].bitcast(FP8X4), lhsT_scale=w_s[b][:],
-                rhs=xw[:].bitcast(FP8X4), rhs_scale=xs[:], start=True, stop=True,
-            )
-            nc.scalar.copy(y[b][:], acc[:])
-
-        cast_w(0)
         cast_w(1)
-        project(0)
-
-        a_bank = [bank(d, "a_bank%d" % d) for d in range(D)]
-        HALF = T // 2
-        a_first = [sb.tile([P, HALF], F32, name="a_first%d" % d) for d in range(D)]
-
-        def a_half(d, h):
-            return a_bank[d][:].rearrange("p (c n) -> p n c", c=PACK)[:, h * 64:(h + 1) * 64, :]
-
-        for d in range(D):
-            for c in range(PACK):
-                nc.tensor.transpose(
-                    a_bank[d][:, c * P:(c + 1) * P], a_small[:, d, c:c + 1].to_broadcast([P, P]), ident[:]
-                )
-            dst = a_first[d][:].rearrange("p (n c) -> p n c", c=PACK)
-            if d == 0:
-                nc.vector.tensor_copy(dst, a_half(d, 0))
-            else:
-                nc.scalar.copy(dst, a_half(d, 0))
-
-        def gather(b, d, v0, width, weights):
-            h = sb.tile([P, width], F32, name="h_%d_%d_%d" % (v0, b, d))
-            nc.vector.tensor_tensor(
-                h[:], y[b][:].indirect(pos[d][:, v0 // 16:(v0 + width) // 16]), weights, ALU.mult
-            )
-            return h
-
-        def turn_add(dst, src, d):
-            nc.tensor.matmul(dst, src, ident[:], start=(d == 0), stop=(d == D - 1), is_transpose=True)
+        project(1)
 
         planes_s = sb.tile([P, T], U8, name="planes_s", align_bytes=64)
         out_rows = out_0.rearrange("(p t) v -> p t v", t=PACK)
         out_words = out_1[0].rearrange("p c r -> p (c r)").bitcast(I32)
-        sums = {c: sb.tile([P, PACK, P], F32, name="sums%d" % c)[:] for c in (2, 3)}
+        words_first = sb.tile([P, 3 * P], U32, name="words_first", align_bytes=64)
+        words_last = sb.tile([P, P], U32, name="words_last", align_bytes=64)
+        LAST = PACK - 1
+        turned = {}
+        backs = {}
+        BACK_BANKS = {0: [7], 1: [5], 2: [6], 3: [7, 5]}
+        gathered = []
 
-        def relu_out(c, src, b0, b1):
+        def gather_turn(b, d, chunks, dsts):
+            gathered.append(None)
+            n = len(gathered)
+            g = sb.tile([P, 2 * P], F32, name="g%d" % n, tag="g%d" % (n % RING))
+            width = P * len(chunks)
+            col = chunks[0] * P // 16
+            nc.vector.tensor_copy(g[:, 0:width], y[b][:].indirect(pos[d][:, col:col + width // 16]))
+            for i, dst in enumerate(dsts):
+                nc.tensor.transpose(dst[:, b * P:(b + 1) * P], g[:, i * P:(i + 1) * P], ident[:])
+            return g
+
+        def turn_bank(c, d):
+            turned[(c, d)] = bank(len(turned) % 5, "turned_%d_%d" % (c, d))
+            return turned[(c, d)]
+
+        def weigh(weighed, src, c, d, b0, b1):
             nc.scalar.activation(
-                sums[c][:, :, 32 * b0:32 * b1],
+                weighed[:, :, 32 * b0:32 * b1],
                 src[:, P * b0:P * b1].rearrange("p (q t) -> p t q", t=PACK),
-                ACT.Relu,
+                ACT.Copy, scale=a[:, d, c:c + 1],
             )
 
-        def finish(c, bank_no, last):
-            back = bank(bank_no, "back%d" % c)
+        seen = {}
+
+        def turn_back(c, weighed):
+            k = seen.get(c, 0)
+            seen[c] = k + 1
+            if k == 0:
+                backs[c] = [bank(i, "back%d_%d" % (c, i)) for i in BACK_BANKS[c]]
+            per = PACK // len(backs[c])
             for t in range(PACK):
-                nc.tensor.transpose(back[:, t * P:(t + 1) * P], sums[c][:, t, :], ident[:])
+                nc.tensor.matmul(
+                    backs[c][t // per][:, (t % per) * P:(t % per + 1) * P], weighed[:, t, :], ident[:],
+                    start=(k == 0 and t % per == 0), stop=(k == D - 1 and t % per == per - 1), is_transpose=True,
+                )
+
+        def weigh_back(c, d):
+            weighed = sb.tile([P, PACK, P], F32, name="weighed_%d_%d" % (c, d))
+            weigh(weighed, turned[(c, d)], c, d, 0, BLOCKS)
+            turn_back(c, weighed)
+
+        def finish(c):
             res = sb.tile([P, PACK, P], F32, name="res%d" % c)
             res_bf = sb.tile([P, P * PACK], BF16, name="res_bf%d" % c, align_bytes=64)
-            words = sb.tile([P, P], U32, name="words%d" % c, align_bytes=64)
             dst = res_bf[:].rearrange("p (v t) -> p v t", t=PACK)
-            src = back[:].rearrange("p (t v) -> p v t", t=PACK)
-            if last:
-                nc.vector.tensor_copy(dst, src)
-            nc.scalar.copy(res[:].rearrange("p t v -> p (t v)"), back[:])
+            flat = res[:].rearrange("p t v -> p (t v)")
+            if c == LAST:
+                nc.scalar.activation(flat[:, 0:2 * P], backs[c][0][:, 0:2 * P], ACT.Relu)
+                nc.vector.tensor_scalar_max(flat[:, 2 * P:], backs[c][1][:, 0:2 * P], 0.0)
+            else:
+                nc.scalar.activation(flat, backs[c][0][:], ACT.Relu)
             nc.sync.dma_start(out=out_rows[:, :, c * P:(c + 1) * P], in_=res[:])
-            if not last:
-                nc.scalar.copy(dst, src)
+            if c >= 2:
+                nc.vector.tensor_copy(dst, res[:].rearrange("p t v -> p v t"))
+            else:
+                nc.scalar.activation(dst, backs[c][0][:].rearrange("p (t v) -> p v t", t=PACK), ACT.Relu)
+            words = words_last[:] if c == LAST else words_first[:, c * P:(c + 1) * P]
             nc.vector.quantize_mx(
-                out=words[:].bitcast(FP8X4), scales=planes_s[:, c * P:(c + 1) * P], in_=res_bf[:]
+                out=words.bitcast(FP8X4), scales=planes_s[:, c * P:(c + 1) * P], in_=res_bf[:]
             )
-            nc.sync.dma_start(out=out_words[:, c * P:(c + 1) * P], in_=words[:].bitcast(I32))
+            if c == LAST - 1:
+                nc.sync.dma_start(out=out_words[:, 0:3 * P], in_=words_first[:].bitcast(I32))
+            if c == LAST:
+                nc.sync.dma_start(out=out_words[:, 3 * P:], in_=words_last[:].bitcast(I32))
 
-        sum_first = []
+        first = [(0, [0, 1]), (1, [0, 1]), (2, [0])]
+        for c, d in [(0, 0), (0, 1), (0, 2), (1, 0), (1, 1)]:
+            turn_bank(c, d)
         for b in range(BLOCKS):
-            if b + 2 < BLOCKS:
-                cast_w(b + 2)
-            if b + 1 < BLOCKS:
+            if 2 <= b + 1 < BLOCKS:
+                cast_w(b + 1)
                 project(b + 1)
-            sum_first.append(bank(3 + (b + 1) % BLOCKS, "sum_first%d" % b))
-            hs = [gather(b, d, 0, HALF, a_first[d][:]) for d in range(D)]
-            for c in range(2):
-                for d in range(D):
-                    turn_add(sum_first[b][:, c * P:(c + 1) * P], hs[d][:, c * P:(c + 1) * P], d)
-            if b + 2 == BLOCKS:
-                a_second = sb.tile([P, D, HALF], F32, name="a_second", tag="late", align_bytes=64)
-                for d in range(D):
-                    nc.scalar.copy(a_second[:, d, :].rearrange("p (n c) -> p n c", c=PACK), a_half(d, 1))
-                sums_first = sb.tile([P, 2, PACK, P], F32, name="sums_first", tag="late2", align_bytes=64)
-                sums[0] = sums_first[:, 0]
-                sums[1] = sums_first[:, 1]
-            for done in ([0, 1, 2] if b + 2 == BLOCKS else [3] if b + 1 == BLOCKS else []):
-                nc.scalar.activation(
-                    sums_first[:, :, :, 32 * done:32 * (done + 1)],
-                    sum_first[done][:, 0:HALF].rearrange("p (c q t) -> p c t q", c=2, t=PACK),
-                    ACT.Relu,
-                )
-        finish(0, 7, False)
-        finish(1, 0, False)
+            for d, chunks in first:
+                g = gather_turn(b, d, chunks, [turned[(c, d)] for c in chunks])
+        for d in range(D):
+            weigh_back(0, d)
+        weigh_back(1, 0)
+        finish(0)
+        weigh_back(1, 1)
 
-        sum2 = bank(3, "sum2")
-        for b in range(BLOCKS):
-            for d in range(D):
-                h = gather(b, d, 2 * P, P, a_second[:, d, 0:P])
-                turn_add(sum2[:, b * P:(b + 1) * P], h[:], d)
-        relu_out(2, sum2, 0, BLOCKS)
-        finish(2, 1, False)
+        for d, chunks in [(2, [1, 2]), (0, [2, 3]), (1, [2, 3])]:
+            dsts = [turn_bank(c, d) for c in chunks]
+            for b in range(BLOCKS):
+                gather_turn(b, d, chunks, dsts)
+            for c in chunks:
+                weigh_back(c, d)
+            if d == 2:
+                finish(1)
 
-        sum3 = bank(3, "sum3")
-        sum3_last = bank(4, "sum3_last")
+        weighed = sb.tile([P, PACK, P], F32, name="weighed_last")
+        most = turn_bank(LAST, 2)
+        rest = turn_bank(LAST, 3)
         for b in range(BLOCKS):
-            for d in range(D):
-                h = gather(b, d, 3 * P, P, a_second[:, d, P:2 * P])
-                dst = sum3_last if b == BLOCKS - 1 else sum3
-                turn_add(dst[:, b * P:(b + 1) * P], h[:], d)
+            g = gather_turn(b, 2, [LAST], [rest if b == BLOCKS - 1 else most])
             if b == BLOCKS - 2:
-                relu_out(3, sum3, 0, BLOCKS - 1)
-        relu_out(3, sum3_last, BLOCKS - 1, BLOCKS)
-        finish(3, 2, True)
+                weigh(weighed, most, LAST, 2, 0, BLOCKS - 1)
+        weigh(weighed, rest, LAST, 2, BLOCKS - 1, BLOCKS)
+        turn_back(LAST, weighed)
+        finish(2)
+        finish(LAST)
 
         for q in range(4):
             eng = nc.scalar if q % 2 else nc.sync

@@ -74,7 +74,7 @@ def tile_picked_wgatv_relu_lo_kernel(
         w_bf = [sb.tile([P, P * PACK], BF16, name="w_bf%d" % b, align_bytes=64) for b in range(BLOCKS)]
         w_q = [sb.tile([P, P], U32, name="w_q%d" % b, align_bytes=64) for b in range(BLOCKS)]
         w_s = [sb.tile([P, P], U8, name="w_s%d" % b, align_bytes=64) for b in range(BLOCKS)]
-        y = [sb.tile([P, T], F32, name="y%d" % b) for b in range(BLOCKS)]
+        y = [sb.tile([P, T], F32, name="y%d" % b, tag="y%d" % b, align_bytes=64) for b in range(BLOCKS)]
 
         def cast_w(b):
             dst = w_bf[b][:].rearrange("p (g i j) -> p g j i", i=4, j=PACK)
@@ -119,7 +119,7 @@ def tile_picked_wgatv_relu_lo_kernel(
         nc.vector.tensor_reduce(den[:], e[:].rearrange("p d c -> p c d"), AXIS.X, ALU.add)
         rden = sb.tile([P, PACK], F32, name="rden")
         nc.vector.reciprocal(rden[:], den[:])
-        a = sb.tile([P, D, PACK], F32, name="a")
+        a = sb.tile([P, D, PACK], F32, name="a", tag="a", align_bytes=64)
         nc.vector.tensor_tensor(a[:], e[:], rden[:].unsqueeze(1).to_broadcast([P, D, PACK]), ALU.mult)
 
         cast_w(1)
@@ -128,12 +128,16 @@ def tile_picked_wgatv_relu_lo_kernel(
         planes_s = sb.tile([P, T], U8, name="planes_s", align_bytes=64)
         out_rows = out_0.rearrange("(p t) v -> p t v", t=PACK)
         out_words = out_1[0].rearrange("p c r -> p (c r)").bitcast(I32)
-        words_first = sb.tile([P, 3 * P], U32, name="words_first", align_bytes=64)
         words_last = sb.tile([P, P], U32, name="words_last", align_bytes=64)
         LAST = PACK - 1
         turned = {}
         backs = {}
-        BACK_BANKS = {0: [7], 1: [5], 2: [6], 3: [7, 5]}
+        BACK_BANKS = {0: [7], 1: [5], 2: [6], 3: [7, 3]}
+        TERMS = {0: 1, 1: 1, 2: 2, 3: 3}
+        ADDS = {0: 2, 1: 2, 2: 1, 3: 0}
+        REUSE = {(1, 2): "total_0_2"}
+        pending = {}
+        added = {c: 0 for c in range(PACK)}
         gathered = []
 
         def gather_turn(b, d, chunks, dsts):
@@ -169,18 +173,36 @@ def tile_picked_wgatv_relu_lo_kernel(
             for t in range(PACK):
                 nc.tensor.matmul(
                     backs[c][t // per][:, (t % per) * P:(t % per + 1) * P], weighed[:, t, :], ident[:],
-                    start=(k == 0 and t % per == 0), stop=(k == D - 1 and t % per == per - 1), is_transpose=True,
+                    start=(k == 0 and t % per == 0), stop=(k == TERMS[c] - 1 and t % per == per - 1), is_transpose=True,
                 )
 
         def weigh_back(c, d):
-            weighed = sb.tile([P, PACK, P], F32, name="weighed_%d_%d" % (c, d))
+            weighed = sb.tile([P, PACK, P], F32, name="weighed_%d_%d" % (c, d), tag=REUSE.get((c, d), "weighed_%d_%d" % (c, d)))
             weigh(weighed, turned[(c, d)], c, d, 0, BLOCKS)
-            turn_back(c, weighed)
+            if c in pending:
+                total = sb.tile([P, PACK, P], F32, name="total_%d_%d" % (c, d), tag="total_%d_%d" % (c, d))
+                nc.gpsimd.tensor_tensor(total[:], pending.pop(c)[:], weighed[:], ALU.add)
+                added[c] = added[c] + 1
+                weighed = total
+            if added[c] < ADDS[c]:
+                pending[c] = weighed
+            else:
+                turn_back(c, weighed)
+
+        results = {}
+        rounded = {}
+
+        def round_result(c, tag):
+            rounded[c] = sb.tile([P, P * PACK], BF16, name="res_bf%d" % c, tag=tag, align_bytes=64)
+            dst = rounded[c][:].rearrange("p (v t) -> p v t", t=PACK)
+            if c >= 2:
+                nc.vector.tensor_copy(dst, results[c][:].rearrange("p t v -> p v t"))
+            else:
+                nc.scalar.activation(dst, backs[c][0][:].rearrange("p (t v) -> p v t", t=PACK), ACT.Relu)
 
         def finish(c):
             res = sb.tile([P, PACK, P], F32, name="res%d" % c)
-            res_bf = sb.tile([P, P * PACK], BF16, name="res_bf%d" % c, align_bytes=64)
-            dst = res_bf[:].rearrange("p (v t) -> p v t", t=PACK)
+            results[c] = res
             flat = res[:].rearrange("p t v -> p (t v)")
             if c == LAST:
                 nc.scalar.activation(flat[:, 0:2 * P], backs[c][0][:, 0:2 * P], ACT.Relu)
@@ -188,21 +210,16 @@ def tile_picked_wgatv_relu_lo_kernel(
             else:
                 nc.scalar.activation(flat, backs[c][0][:], ACT.Relu)
             nc.sync.dma_start(out=out_rows[:, :, c * P:(c + 1) * P], in_=res[:])
-            if c >= 2:
-                nc.vector.tensor_copy(dst, res[:].rearrange("p t v -> p v t"))
-            else:
-                nc.scalar.activation(dst, backs[c][0][:].rearrange("p (t v) -> p v t", t=PACK), ACT.Relu)
-            words = words_last[:] if c == LAST else words_first[:, c * P:(c + 1) * P]
-            nc.vector.quantize_mx(
-                out=words.bitcast(FP8X4), scales=planes_s[:, c * P:(c + 1) * P], in_=res_bf[:]
-            )
-            if c == LAST - 1:
-                nc.sync.dma_start(out=out_words[:, 0:3 * P], in_=words_first[:].bitcast(I32))
-            if c == LAST:
-                nc.sync.dma_start(out=out_words[:, 3 * P:], in_=words_last[:].bitcast(I32))
+            if c < 2:
+                round_result(c, "rounded%d" % c)
 
-        first = [(0, [0, 1]), (1, [0, 1]), (2, [0])]
-        for c, d in [(0, 0), (0, 1), (0, 2), (1, 0), (1, 1)]:
+        def quantise(c, words):
+            nc.vector.quantize_mx(
+                out=words.bitcast(FP8X4), scales=planes_s[:, c * P:(c + 1) * P], in_=rounded[c][:]
+            )
+
+        first = [(0, [0, 1]), (1, [0]), (2, [0])]
+        for c, d in [(0, 0), (0, 1), (0, 2), (1, 0)]:
             turn_bank(c, d)
         for b in range(BLOCKS):
             if 2 <= b + 1 < BLOCKS:
@@ -214,16 +231,15 @@ def tile_picked_wgatv_relu_lo_kernel(
             weigh_back(0, d)
         weigh_back(1, 0)
         finish(0)
-        weigh_back(1, 1)
 
-        for d, chunks in [(2, [1, 2]), (0, [2, 3]), (1, [2, 3])]:
+        for d, chunks, done in [(1, [1, 2], None), (2, [1, 2], 1), (0, [2, 3], None), (1, [3], 2)]:
             dsts = [turn_bank(c, d) for c in chunks]
             for b in range(BLOCKS):
                 gather_turn(b, d, chunks, dsts)
             for c in chunks:
                 weigh_back(c, d)
-            if d == 2:
-                finish(1)
+            if done is not None:
+                finish(done)
 
         weighed = sb.tile([P, PACK, P], F32, name="weighed_last")
         most = turn_bank(LAST, 2)
@@ -232,10 +248,19 @@ def tile_picked_wgatv_relu_lo_kernel(
             g = gather_turn(b, 2, [LAST], [rest if b == BLOCKS - 1 else most])
             if b == BLOCKS - 2:
                 weigh(weighed, most, LAST, 2, 0, BLOCKS - 1)
-        weigh(weighed, rest, LAST, 2, BLOCKS - 1, BLOCKS)
+        nc.vector.tensor_scalar_mul(
+            weighed[:, :, 32 * LAST:], rest[:, P * LAST:].rearrange("p (q t) -> p t q", t=PACK), a[:, 2, LAST:LAST + 1]
+        )
         turn_back(LAST, weighed)
-        finish(2)
+        words_first = sb.tile([P, 3 * P], U32, name="words_first", tag="y3", align_bytes=64)
+        round_result(2, "a")
+        for c in range(LAST):
+            quantise(c, words_first[:, c * P:(c + 1) * P])
+        nc.sync.dma_start(out=out_words[:, 0:3 * P], in_=words_first[:].bitcast(I32))
         finish(LAST)
+        round_result(LAST, "rounded3")
+        quantise(LAST, words_last[:])
+        nc.sync.dma_start(out=out_words[:, 3 * P:], in_=words_last[:].bitcast(I32))
 
         for q in range(4):
             eng = nc.scalar if q % 2 else nc.sync

@@ -13,6 +13,10 @@ BYTES = K * T + K * T // 32 + 4 * K * N + 4 * D * T + D * P * (T // 16) * 2 + 4 
 ROW_STEP = 9
 D_STEP = 60
 RING = 4
+STEPS = [(1, [1, 2], None), (2, [1], 1), (0, [2, 3], None), (2, [2], 2), (1, [3], None)]
+TURN_BANKS = [0, 1, 2, 3, 4, 0, 6, 0, 4, 7, 3, 0, 5]
+BACK_BANKS = {0: [7], 1: [5], 2: [6], 3: [2, 4]}
+ADDS = {0: 1, 1: 2, 2: 2, 3: 0}
 
 F32 = mybir.dt.float32
 BF16 = mybir.dt.bfloat16
@@ -132,10 +136,8 @@ def tile_picked_wgatv_relu_lo_kernel(
         LAST = PACK - 1
         turned = {}
         backs = {}
-        BACK_BANKS = {0: [7], 1: [5], 2: [6], 3: [7, 3]}
-        TERMS = {0: 1, 1: 1, 2: 2, 3: 3}
-        ADDS = {0: 2, 1: 2, 2: 1, 3: 0}
-        REUSE = {(1, 2): "total_0_2"}
+        TERMS = {c: D - ADDS[c] for c in range(LAST)}
+        TERMS[LAST] = 2
         pending = {}
         added = {c: 0 for c in range(PACK)}
         gathered = []
@@ -152,7 +154,7 @@ def tile_picked_wgatv_relu_lo_kernel(
             return g
 
         def turn_bank(c, d):
-            turned[(c, d)] = bank(len(turned) % 5, "turned_%d_%d" % (c, d))
+            turned[(c, d)] = bank(TURN_BANKS[len(turned)], "turned_%d_%d" % (c, d))
             return turned[(c, d)]
 
         def weigh(weighed, src, c, d, b0, b1):
@@ -177,14 +179,14 @@ def tile_picked_wgatv_relu_lo_kernel(
                 )
 
         def weigh_back(c, d):
-            weighed = sb.tile([P, PACK, P], F32, name="weighed_%d_%d" % (c, d), tag=REUSE.get((c, d), "weighed_%d_%d" % (c, d)))
+            weighed = sb.tile([P, PACK, P], F32, name="weighed_%d_%d" % (c, d))
             weigh(weighed, turned[(c, d)], c, d, 0, BLOCKS)
             if c in pending:
                 total = sb.tile([P, PACK, P], F32, name="total_%d_%d" % (c, d), tag="total_%d_%d" % (c, d))
                 nc.gpsimd.tensor_tensor(total[:], pending.pop(c)[:], weighed[:], ALU.add)
                 added[c] = added[c] + 1
                 weighed = total
-            if added[c] < ADDS[c]:
+            if added[c] < ADDS[c] or (c, d) == (LAST, 1):
                 pending[c] = weighed
             else:
                 turn_back(c, weighed)
@@ -222,9 +224,9 @@ def tile_picked_wgatv_relu_lo_kernel(
         for c, d in [(0, 0), (0, 1), (0, 2), (1, 0)]:
             turn_bank(c, d)
         for b in range(BLOCKS):
-            if 2 <= b + 1 < BLOCKS:
-                cast_w(b + 1)
-                project(b + 1)
+            if b + 2 < BLOCKS:
+                cast_w(b + 2)
+                project(b + 2)
             for d, chunks in first:
                 g = gather_turn(b, d, chunks, [turned[(c, d)] for c in chunks])
         for d in range(D):
@@ -232,7 +234,7 @@ def tile_picked_wgatv_relu_lo_kernel(
         weigh_back(1, 0)
         finish(0)
 
-        for d, chunks, done in [(1, [1, 2], None), (2, [1, 2], 1), (0, [2, 3], None), (1, [3], 2)]:
+        for d, chunks, done in STEPS:
             dsts = [turn_bank(c, d) for c in chunks]
             for b in range(BLOCKS):
                 gather_turn(b, d, chunks, dsts)
@@ -242,15 +244,16 @@ def tile_picked_wgatv_relu_lo_kernel(
                 finish(done)
 
         weighed = sb.tile([P, PACK, P], F32, name="weighed_last")
-        most = turn_bank(LAST, 2)
-        rest = turn_bank(LAST, 3)
+        halves = [turn_bank(LAST, 2), turn_bank(LAST, 3)]
         for b in range(BLOCKS):
-            g = gather_turn(b, 2, [LAST], [rest if b == BLOCKS - 1 else most])
-            if b == BLOCKS - 2:
-                weigh(weighed, most, LAST, 2, 0, BLOCKS - 1)
-        nc.vector.tensor_scalar_mul(
-            weighed[:, :, 32 * LAST:], rest[:, P * LAST:].rearrange("p (q t) -> p t q", t=PACK), a[:, 2, LAST:LAST + 1]
-        )
+            gather_turn(b, 2, [LAST], [halves[b // 2]])
+        partial = pending.pop(LAST)
+        for u in range(2):
+            nc.vector.scalar_tensor_tensor(
+                weighed[:, :, 64 * u:64 * (u + 1)],
+                halves[u][:, 2 * P * u:2 * P * (u + 1)].rearrange("p (q t) -> p t q", t=PACK),
+                a[:, 2, LAST:LAST + 1], partial[:, :, 64 * u:64 * (u + 1)], ALU.mult, ALU.add,
+            )
         turn_back(LAST, weighed)
         words_first = sb.tile([P, 3 * P], U32, name="words_first", tag="y3", align_bytes=64)
         round_result(2, "a")

from contextlib import ExitStack

import concourse.mybir as mybir
from concourse.masks import make_identity

K, T, D, N = 512, 512, 3, 512
P = 128
PACK = 4
BLOCKS = N // P
FLOPS = 2 * K * T * N
BYTES = K * T + K * T // 32 + 4 * K * N + 4 * D * T + D * P * (T // 16) * 2 + 4 * N * T + N * T + N * T // 32

ROW_STEP = 9
D_STEP = 60
RING = 4
STEPS = [(1, [1, 2], None), (2, [1], 1), (0, [2, 3], None), (2, [2], 2), (1, [3], None)]
TURN_BANKS = [0, 1, 2, 3, 4, 0, 6, 0, 4, 7, 3, 0, 5]
BACK_BANKS = {0: [7], 1: [5], 2: [6], 3: [2, 4]}
ADDS = {0: 1, 1: 2, 2: 2, 3: 0}

F32 = mybir.dt.float32
BF16 = mybir.dt.bfloat16
I32 = mybir.dt.int32
U32 = mybir.dt.uint32
U16 = mybir.dt.uint16
U8 = mybir.dt.uint8
FP8X4 = mybir.dt.float8_e4m3fn_x4
ALU = mybir.AluOpType
ACT = mybir.ActivationFunctionType
AXIS = mybir.AxisListType


def tile_picked_wgatv_relu_lo_kernel(
    tc, x_words, x_scales, w1, score, pos1, pos2, pos3, out_0, out_1, out_2
):
    nc = tc.nc
    with ExitStack() as ctx:
        sb = ctx.enter_context(tc.tile_pool(name="sb", bufs=1))
        ps = ctx.enter_context(tc.psum_pool(name="ps", bufs=1))

        def bank(i, name):
            return ps.tile([P, T], F32, name=name, tag="bank%d" % i)

        s_rows = sb.tile([P, P], F32, name="s_rows")
        nc.gpsimd.dma_start(
            out=s_rows[:], in_=score.rearrange("d p (c n) -> (d p c) n", n=P)[0:ROW_STEP * P:ROW_STEP, :]
        )
        w_raw = [sb.tile([P, PACK, P], F32, name="w_raw%d" % b) for b in range(BLOCKS)]

        def load_w(b):
            nc.sync.dma_start(out=w_raw[b][:], in_=w1[:, b * P:(b + 1) * P].rearrange("(p j) m -> p j m", j=PACK))

        load_w(0)
        xw = sb.tile([P, T], U32, name="xw", align_bytes=64)
        nc.sync.dma_start(out=xw[:].bitcast(I32), in_=x_words[0].rearrange("p c r -> p (c r)").bitcast(I32))
        xs = sb.tile([P, T], U8, name="xs", align_bytes=64)
        for q in range(4):
            nc.scalar.dma_start(
                out=xs[32 * q:32 * (q + 1), :].bitcast(I32),
                in_=x_scales[0, 4 * q:4 * (q + 1), :].bitcast(I32).partition_broadcast(8),
            )
        pos = [sb.tile([P, T // 16], U16, name="pos%d" % d) for d in range(D)]
        nc.sync.dma_start(pos[0][:], pos1)
        load_w(1)
        load_w(2)
        load_w(3)
        nc.sync.dma_start(pos[1][:], pos2)
        nc.sync.dma_start(pos[2][:], pos3)

        ident = sb.tile([P, P], F32, name="ident")
        make_identity(nc, ident[:])

        warm_in = sb.tile([P, 1], F32, name="warm_in")
        warm_out = sb.tile([P, 1], F32, name="warm_out")
        nc.vector.memset(warm_in[:], 0.0)
        nc.scalar.activation(warm_out[:], warm_in[:], ACT.Exp)

        w_bf = [sb.tile([P, P * PACK], BF16, name="w_bf%d" % b, align_bytes=64) for b in range(BLOCKS)]
        w_q = [sb.tile([P, P], U32, name="w_q%d" % b, align_bytes=64) for b in range(BLOCKS)]
        w_s = [sb.tile([P, P], U8, name="w_s%d" % b, align_bytes=64) for b in range(BLOCKS)]
        y = [sb.tile([P, T], F32, name="y%d" % b, tag="y%d" % b, align_bytes=64) for b in range(BLOCKS)]

        def cast_w(b):
            dst = w_bf[b][:].rearrange("p (g i j) -> p g j i", i=4, j=PACK)
            src = w_raw[b][:].rearrange("p j (g i) -> p g j i", i=4)
            if b < 2:
                nc.vector.tensor_copy(dst, src)
            else:
                nc.scalar.copy(dst, src)

        def product(acc, b, cols):
            nc.tensor.matmul_mx(
                out=acc, lhsT=w_q[b][:].bitcast(FP8X4), lhsT_scale=w_s[b][:],
                rhs=xw[:, cols].bitcast(FP8X4), rhs_scale=xs[:, cols], start=True, stop=True,
            )

        def project(b):
            nc.vector.quantize_mx(out=w_q[b][:].bitcast(FP8X4), scales=w_s[b][:], in_=w_bf[b][:])
            if b == 0:
                for h, copy in enumerate((nc.scalar.copy, nc.vector.tensor_copy)):
                    cols = slice(h * T // 2, (h + 1) * T // 2)
                    acc = bank(5 + h, "acc0_%d" % h)
                    product(acc[:, 0:T // 2], b, cols)
                    copy(y[b][:, cols], acc[:, 0:T // 2])
            else:
                acc = bank(5 + (b + 1) % 2, "acc%d" % b)
                product(acc[:], b, slice(0, T))
                nc.scalar.copy(y[b][:], acc[:])

        cast_w(0)
        project(0)

        s_bank = bank(7, "s_bank")
        nc.tensor.transpose(s_bank[:, 0:P], s_rows[:], ident[:])
        s_dc = s_bank[:, 0:D * D_STEP].rearrange("p (d r) -> p d r", r=D_STEP)[:, :, 0:PACK]
        top = sb.tile([P, PACK], F32, name="top")
        nc.vector.tensor_reduce(top[:], s_dc.rearrange("p d c -> p c d"), AXIS.X, ALU.max)
        z = sb.tile([P, D, PACK], F32, name="z")
        nc.vector.tensor_tensor(z[:], s_dc, top[:].unsqueeze(1).to_broadcast([P, D, PACK]), ALU.subtract)
        e = sb.tile([P, D, PACK], F32, name="e")
        nc.scalar.activation(e[:], z[:], ACT.Exp)
        den = sb.tile([P, PACK], F32, name="den")
        nc.vector.tensor_reduce(den[:], e[:].rearrange("p d c -> p c d"), AXIS.X, ALU.add)
        rden = sb.tile([P, PACK], F32, name="rden")
        nc.vector.reciprocal(rden[:], den[:])
        a = sb.tile([P, D, PACK], F32, name="a", tag="a", align_bytes=64)
        nc.vector.tensor_tensor(a[:], e[:], rden[:].unsqueeze(1).to_broadcast([P, D, PACK]), ALU.mult)

        cast_w(1)
        project(1)

        planes_s = sb.tile([P, T], U8, name="planes_s", align_bytes=64)
        out_rows = out_0.rearrange("(p t) v -> p t v", t=PACK)
        out_words = out_1[0].rearrange("p c r -> p (c r)").bitcast(I32)
        words_last = sb.tile([P, P], U32, name="words_last", align_bytes=64)
        LAST = PACK - 1
        turned = {}
        backs = {}
        TERMS = {c: D - ADDS[c] for c in range(LAST)}
        TERMS[LAST] = 2
        pending = {}
        added = {c: 0 for c in range(PACK)}
        gathered = []

        def gather_turn(b, d, chunks, dsts):
            gathered.append(None)
            n = len(gathered)
            g = sb.tile([P, 2 * P], F32, name="g%d" % n, tag="g%d" % (n % RING))
            width = P * len(chunks)
            col = chunks[0] * P // 16
            nc.vector.tensor_copy(g[:, 0:width], y[b][:].indirect(pos[d][:, col:col + width // 16]))
            for i, dst in enumerate(dsts):
                nc.tensor.transpose(dst[:, b * P:(b + 1) * P], g[:, i * P:(i + 1) * P], ident[:])
            return g

        def turn_bank(c, d):
            turned[(c, d)] = bank(TURN_BANKS[len(turned)], "turned_%d_%d" % (c, d))
            return turned[(c, d)]

        def weigh(weighed, src, c, d, b0, b1):
            nc.scalar.activation(
                weighed[:, :, 32 * b0:32 * b1],
                src[:, P * b0:P * b1].rearrange("p (q t) -> p t q", t=PACK),
                ACT.Copy, scale=a[:, d, c:c + 1],
            )

        seen = {}

        def turn_back(c, weighed):
            k = seen.get(c, 0)
            seen[c] = k + 1
            if k == 0:
                backs[c] = [bank(i, "back%d_%d" % (c, i)) for i in BACK_BANKS[c]]
            per = PACK // len(backs[c])
            for t in range(PACK):
                nc.tensor.matmul(
                    backs[c][t // per][:, (t % per) * P:(t % per + 1) * P], weighed[:, t, :], ident[:],
                    start=(k == 0 and t % per == 0), stop=(k == TERMS[c] - 1 and t % per == per - 1), is_transpose=True,
                )

        def weigh_back(c, d):
            weighed = sb.tile([P, PACK, P], F32, name="weighed_%d_%d" % (c, d))
            weigh(weighed, turned[(c, d)], c, d, 0, BLOCKS)
            if c in pending:
                total = sb.tile([P, PACK, P], F32, name="total_%d_%d" % (c, d), tag="total_%d_%d" % (c, d))
                nc.gpsimd.tensor_tensor(total[:], pending.pop(c)[:], weighed[:], ALU.add)
                added[c] = added[c] + 1
                weighed = total
            if added[c] < ADDS[c] or (c, d) == (LAST, 1):
                pending[c] = weighed
            else:
                turn_back(c, weighed)

        results = {}
        rounded = {}

        def round_result(c, tag):
            rounded[c] = sb.tile([P, P * PACK], BF16, name="res_bf%d" % c, tag=tag, align_bytes=64)
            dst = rounded[c][:].rearrange("p (v t) -> p v t", t=PACK)
            if c >= 2:
                nc.vector.tensor_copy(dst, results[c][:].rearrange("p t v -> p v t"))
            else:
                nc.scalar.activation(dst, backs[c][0][:].rearrange("p (t v) -> p v t", t=PACK), ACT.Relu)

        def finish(c):
            res = sb.tile([P, PACK, P], F32, name="res%d" % c)
            results[c] = res
            flat = res[:].rearrange("p t v -> p (t v)")
            if c == LAST:
                nc.scalar.activation(flat[:, 0:2 * P], backs[c][0][:, 0:2 * P], ACT.Relu)
                nc.vector.tensor_scalar_max(flat[:, 2 * P:], backs[c][1][:, 0:2 * P], 0.0)
            else:
                nc.scalar.activation(flat, backs[c][0][:], ACT.Relu)
            nc.sync.dma_start(out=out_rows[:, :, c * P:(c + 1) * P], in_=res[:])
            if c < 2:
                round_result(c, "rounded%d" % c)

        def quantise(c, words):
            nc.vector.quantize_mx(
                out=words.bitcast(FP8X4), scales=planes_s[:, c * P:(c + 1) * P], in_=rounded[c][:]
            )

        first = [(0, [0, 1]), (1, [0]), (2, [0])]
        for c, d in [(0, 0), (0, 1), (0, 2), (1, 0)]:
            turn_bank(c, d)
        for b in range(BLOCKS):
            if b + 2 < BLOCKS:
                cast_w(b + 2)
                project(b + 2)
            for d, chunks in first:
                g = gather_turn(b, d, chunks, [turned[(c, d)] for c in chunks])
        for d in range(D):
            weigh_back(0, d)
        weigh_back(1, 0)
        finish(0)

        for d, chunks, done in STEPS:
            dsts = [turn_bank(c, d) for c in chunks]
            for b in range(BLOCKS):
                gather_turn(b, d, chunks, dsts)
            for c in chunks:
                weigh_back(c, d)
            if done is not None:
                finish(done)

        weighed = sb.tile([P, PACK, P], F32, name="weighed_last")
        halves = [turn_bank(LAST, 2), turn_bank(LAST, 3)]
        for b in range(BLOCKS):
            gather_turn(b, 2, [LAST], [halves[b // 2]])
        partial = pending.pop(LAST)
        for u in range(2):
            nc.vector.scalar_tensor_tensor(
                weighed[:, :, 64 * u:64 * (u + 1)],
                halves[u][:, 2 * P * u:2 * P * (u + 1)].rearrange("p (q t) -> p t q", t=PACK),
                a[:, 2, LAST:LAST + 1], partial[:, :, 64 * u:64 * (u + 1)], ALU.mult, ALU.add,
            )
        turn_back(LAST, weighed)
        words_first = sb.tile([P, 3 * P], U32, name="words_first", tag="y3", align_bytes=64)
        round_result(2, "a")
        for c in range(LAST):
            quantise(c, words_first[:, c * P:(c + 1) * P])
        nc.sync.dma_start(out=out_words[:, 0:3 * P], in_=words_first[:].bitcast(I32))
        finish(LAST)
        round_result(LAST, "rounded3")
        quantise(LAST, words_last[:])
        nc.sync.dma_start(out=out_words[:, 3 * P:], in_=words_last[:].bitcast(I32))

        for q in range(4):
            eng = nc.scalar if q % 2 else nc.sync
            eng.dma_start(
                out=out_2[0, 4 * q:4 * (q + 1), :].bitcast(I32),
                in_=planes_s[32 * q:32 * q + 4, :].bitcast(I32),
            )
